import numpy as np, ml_dtypes
CORES = [71,199,95,223,103,231,111,239,119,247,127,255]
N = 12
K, F = 4, 64
def setup_inputs(rng):
    return {"gr": rng.standard_normal((N, K, 128, N * F), dtype=np.float32).astype(ml_dtypes.bfloat16)}
def setup_inputs_big(rng):
    d = setup_inputs(rng)
    for k in ("gr",): d[k] = (d[k].astype(np.float32) * 1048576.0).astype(d[k].dtype)
    return d
def setup_inputs_small(rng):
    d = setup_inputs(rng)
    for k in ("gr",): d[k] = (d[k].astype(np.float32) * (1 / 1048576.0)).astype(d[k].dtype)
    return d
def reference(gr):
    s = gr.astype(np.float64).sum(axis=(0, 1))
    return {"y": np.stack([s[:, F * r:F * r + F] for r in range(N)]).astype(np.float32 if gr.dtype != np.float64 else np.float64)}

@@ -1,0 +1,118 @@
+from concourse.bass import DstId, RemoteDMATransfer
+from concourse.mybir import AluOpType
+
+N, K, F = 12, 4, 64
+W = N * F
+CH = 2 * F
+NCH = N // 2
+
+SCRATCH = {
+    "tab": ("sbuf", [128, K * W], "bfloat16"),
+    "part": ("sbuf", [128, W], "float32"),
+    "land": ("sbuf", [128, W], "float32"),
+    "acc": ("sbuf", [128, F], "float32"),
+    "ps": ("psum", [128, 1024], "float32"),
+}
+
+SEMAPHORES = (["sent", "vp", "vc", "st"]
+              + ["ld%d" % k for k in range(K)]
+              + ["sv%d" % c for c in range(NCH)]
+              + ["ar%d" % s for s in range(N)])
+
+
+def _bits(m):
+    return [e for e in range(m.bit_length()) if (m >> e) & 1]
+
+
+def _mask(engines):
+    m = 0
+    for e in engines:
+        m |= 1 << e
+    return m
+
+
+def _round(rank):
+    own = rank // 2
+    return [(own + j) % NCH for j in range(1, NCH)] + [own]
+
+
+def rank_program(g, core, T, topo):
+    rank = T.rank_of(core)
+    if rank is None:
+        return
+    v, sy, sc, sem = g.vector, g.sync, g.scalar, T.sem
+    own = rank // 2
+    order = _round(rank)
+    add = AluOpType.add
+
+    def cols(c):
+        return slice(c * CH, (c + 1) * CH)
+
+    def tcols(k, c):
+        return slice(k * W + c * CH, k * W + (c + 1) * CH)
+
+    def blk(r):
+        return slice(r * F, (r + 1) * F)
+
+    for k in range(K):
+        (sy, sc)[k % 2].dma_start(out=T.tab[:, k * W:(k + 1) * W], in_=T.gr[k]).then_inc(sem["ld%d" % k], 16)
+
+    nvp = 0
+    for i, c in enumerate(order):
+        if i == 0:
+            v.wait_ge(sem.ld0, 16)
+            v.wait_ge(sem.ld1, 16)
+        v.tensor_tensor(T.ps[:, cols(c)], T.tab[:, tcols(0, c)], T.tab[:, tcols(1, c)], add).then_inc(sem.vp, 1)
+        nvp += 1
+        if i == 0:
+            v.wait_ge(sem.ld2, 16)
+        v.wait_ge(sem.vp, nvp)
+        v.tensor_tensor(T.ps[:, cols(c)], T.ps[:, cols(c)], T.tab[:, tcols(2, c)], add).then_inc(sem.vp, 1)
+        nvp += 1
+        if i == 0:
+            v.wait_ge(sem.ld3, 16)
+        v.wait_ge(sem.vp, nvp)
+        v.tensor_tensor(T.part[:, cols(c)], T.ps[:, cols(c)], T.tab[:, tcols(3, c)], add).then_inc(sem["sv%d" % c], 1)
+
+    sent = 0
+    for c in order[:-1]:
+        dsts = [2 * c, 2 * c + 1]
+        eng = _bits(topo.mask(core, T.cores[dsts[0]]) & topo.mask(core, T.cores[dsts[1]]))
+        half = len(eng) // 2
+        trs = []
+        for i, d in enumerate(dsts):
+            rid, pid = topo.addr(T.cores[d], core)
+            trs.append(RemoteDMATransfer(dst_ids=[DstId(rid=rid, pnc=pid)],
+                                         dma_engine_mask=_mask(eng[i * half:(i + 1) * half]),
+                                         remote_sem=sem["ar%d" % rank],
+                                         src=T.part[:, blk(d)], dst=T.land[:, blk(rank)]))
+            sent += half
+        g.wait_ge(sem["sv%d" % c], 1)
+        g.remote_dma_fused(trs, local_sem=sem.sent)
+    sib = rank ^ 1
+    rid, pid = topo.addr(T.cores[sib], core)
+    m = topo.mask(core, T.cores[sib])
+    g.wait_ge(sem["sv%d" % own], 1)
+    g.remote_dma(out_ap=T.land[:, blk(rank)], in_ap=T.part[:, blk(sib)], remote_sem=sem["ar%d" % rank],
+                 local_sem=sem.sent, pid=pid, routing_id=rid, dma_engine_mask=m)
+    sent += len(_bits(m))
+
+    arrivals = []
+    for j in range(1, NCH):
+        cs = (own - j) % NCH
+        for s in (2 * cs, 2 * cs + 1):
+            e = _bits(topo.mask(T.cores[s], T.cores[2 * own]) & topo.mask(T.cores[s], T.cores[2 * own + 1]))
+            arrivals.append((s, len(e) // 2))
+    arrivals.append((sib, len(_bits(topo.mask(T.cores[sib], core)))))
+    run = T.ps[:, W:W + F]
+    v.wait_ge(sem["sv%d" % own], 1)
+    for i, (s, n) in enumerate(arrivals):
+        v.wait_ge(sem["ar%d" % s], n)
+        if i:
+            v.wait_ge(sem.vc, i)
+        v.tensor_tensor(T.acc[:, :] if i == len(arrivals) - 1 else run, run if i else T.part[:, blk(rank)],
+                        T.land[:, blk(s)], add).then_inc(sem.vc, 1)
+    sy.wait_ge(sem.vc, len(arrivals))
+    sy.dma_start(out=T.y[:, :], in_=T.acc[:, :]).then_inc(sem.st, 16)
+    sy.wait_ge(sem.st, 16)
+    g.wait_ge(sem.sent, sent)

@@ -5,18 +5,28 @@ N, K, F = 12, 4, 64
 W = N * F
 CH = 2 * F
 NCH = N // 2
+HP = NCH // 2
+HW = HP * CH
+BANK = 512
+NU = 8
+NV = 3
+NH1 = 4
+B = 32
 
 SCRATCH = {
     "tab": ("sbuf", [128, K * W], "bfloat16"),
+    "seed": ("sbuf", [128, B * B], "bfloat16"),
+    "eye": ("sbuf", [128, 128], "bfloat16"),
     "part": ("sbuf", [128, W], "float32"),
     "land": ("sbuf", [128, W], "float32"),
     "acc": ("sbuf", [128, F], "float32"),
-    "ps": ("psum", [128, 1024], "float32"),
+    "ps": ("psum", [128, (1 + NU - NV) * BANK], "float32"),
 }
 
-SEMAPHORES = (["sent", "vp", "vc", "st"]
-              + ["ld%d" % k for k in range(K)]
-              + ["sv%d" % c for c in range(NCH)]
+SEMAPHORES = (["ms", "ey", "sent", "vp", "vc", "st"]
+              + ["ld%d%d" % (h, k) for h in range(2) for k in range(K)]
+              + ["pe%d" % u for u in range(NU)]
+              + ["sv%d" % u for u in range(NU)]
               + ["ar%d" % s for s in range(N)])
 
 
@@ -31,82 +41,136 @@ def _mask(engines):
     return m
 
 
-def _round(rank):
+def _dests(rank):
     own = rank // 2
-    return [(own + j) % NCH for j in range(1, NCH)] + [own]
+    mine, p = own // HP, own % HP
+    far = [HP * (1 - mine) + (p + j) % HP for j in range(HP)]
+    near = [HP * mine + (p + j) % HP for j in range(1, HP)]
+    first = 2 * far[0] + rank % 2
+    return ([[first], [first ^ 1]] + [[2 * c, 2 * c + 1] for c in far[1:] + near] + [[rank ^ 1], [rank]])
+
+
+def _plan(rank, T, topo):
+    core = T.cores[rank]
+    m = None
+    for d in range(N):
+        if d != rank:
+            m = topo.mask(core, T.cores[d]) if m is None else m & topo.mask(core, T.cores[d])
+    eng = _bits(m)
+    h = len(eng) // 2
+    out = []
+    for u, ds in enumerate(_dests(rank)[:-1]):
+        out.append((u, [(ds[0], eng)] if len(ds) == 1 else [(ds[0], eng[:h]), (ds[1], eng[h:])]))
+    return out
+
+
+def _finish(plan):
+    busy, out = {}, {}
+    for _u, trs in plan:
+        for d, es in trs:
+            t = max(busy.get(e, 0) for e in es) + 128 // len(es)
+            for e in es:
+                busy[e] = t
+            out[d] = (t, len(es))
+    return out
 
 
 def rank_program(g, core, T, topo):
     rank = T.rank_of(core)
     if rank is None:
         return
-    v, sy, sc, sem = g.vector, g.sync, g.scalar, T.sem
-    own = rank // 2
-    order = _round(rank)
+    v, pe, sy, sc, sem = g.vector, g.tensor, g.sync, g.scalar, T.sem
     add = AluOpType.add
-
-    def cols(c):
-        return slice(c * CH, (c + 1) * CH)
-
-    def tcols(k, c):
-        return slice(k * W + c * CH, k * W + (c + 1) * CH)
+    units = [(min(ds) * F, len(ds) * F) for ds in _dests(rank)]
+    halves = [1 - (rank // 2) // HP, (rank // 2) // HP]
 
     def blk(r):
         return slice(r * F, (r + 1) * F)
 
-    for k in range(K):
-        (sy, sc)[k % 2].dma_start(out=T.tab[:, k * W:(k + 1) * W], in_=T.gr[k]).then_inc(sem["ld%d" % k], 16)
+    def tab(k, u):
+        a, w = units[u]
+        return T.tab[:, k * W + a:k * W + a + w]
 
-    nvp = 0
-    for i, c in enumerate(order):
-        if i == 0:
-            v.wait_ge(sem.ld0, 16)
-            v.wait_ge(sem.ld1, 16)
-        v.tensor_tensor(T.ps[:, cols(c)], T.tab[:, tcols(0, c)], T.tab[:, tcols(1, c)], add).then_inc(sem.vp, 1)
+    def part(u):
+        a, w = units[u]
+        return T.part[:, a:a + w]
+
+    v.memset(T.seed[0:1, :], 0.0).then_inc(sem.ms, 1)
+    v.memset(T.eye[:, :], 0.0).then_inc(sem.ms, 1)
+    v.wait_ge(sem.ms, 2)
+    v.memset(T.seed[0:1, 0:B * B:B + 1], 1.0).then_inc(sem.ms, 1)
+    for i, h in enumerate(halves):
+        for k in range(K):
+            (sy, sc)[k % 2].dma_start(out=T.tab[:, k * W + h * HW:k * W + (h + 1) * HW],
+                                      in_=T.gr[k, :, h * HW:(h + 1) * HW]).then_inc(sem["ld%d%d" % (i, k)], 16)
+    sy.wait_ge(sem.ms, 3)
+    sc.wait_ge(sem.ms, 3)
+    nb = 128 // B
+    for i in range(nb):
+        (sy, sc)[i % 2].dma_start(out=T.eye[i * B:(i + 1) * B, i * B:(i + 1) * B],
+                                  in_=T.seed[0:1, :]).then_inc(sem.ey, 16)
+
+    def bank(u):
+        a = (1 + u - NV) * BANK
+        return T.ps[:, a:a + units[u][1]]
+
+    pe.wait_ge(sem.ey, 16 * nb)
+    for k in range(K - 1):
+        pe.wait_ge(sem["ld0%d" % k], 16)
+    for u in range(NV, NU):
+        if u == NH1:
+            for k in range(K - 1):
+                pe.wait_ge(sem["ld1%d" % k], 16)
+        for k in range(K - 1):
+            mm = pe.matmul(bank(u), T.eye[:, :], tab(k, u), start=(k == 0), stop=(k == K - 2))
+        mm.then_inc(sem["pe%d" % u], 1)
+
+    nvp, off = 0, 0
+    for u in range(NV):
+        w = units[u][1]
+        p = T.ps[:, off:off + w]
+        off += w
+        if u == 0:
+            v.wait_ge(sem.ld00, 16)
+            v.tensor_copy(p, tab(0, u)).then_inc(sem.vp, 1)
+            nvp += 1
+            v.wait_ge(sem.ld01, 16)
+            v.wait_ge(sem.vp, nvp)
+            v.tensor_tensor(p, p, tab(1, u), add).then_inc(sem.vp, 1)
+        else:
+            v.tensor_tensor(p, tab(0, u), tab(1, u), add).then_inc(sem.vp, 1)
         nvp += 1
-        if i == 0:
-            v.wait_ge(sem.ld2, 16)
+        if u == 0:
+            v.wait_ge(sem.ld02, 16)
         v.wait_ge(sem.vp, nvp)
-        v.tensor_tensor(T.ps[:, cols(c)], T.ps[:, cols(c)], T.tab[:, tcols(2, c)], add).then_inc(sem.vp, 1)
+        v.tensor_tensor(p, p, tab(2, u), add).then_inc(sem.vp, 1)
         nvp += 1
-        if i == 0:
-            v.wait_ge(sem.ld3, 16)
+        if u == 0:
+            v.wait_ge(sem.ld03, 16)
         v.wait_ge(sem.vp, nvp)
-        v.tensor_tensor(T.part[:, cols(c)], T.ps[:, cols(c)], T.tab[:, tcols(3, c)], add).then_inc(sem["sv%d" % c], 1)
+        v.tensor_tensor(part(u), p, tab(3, u), add).then_inc(sem["sv%d" % u], 1)
+    for u in range(NV, NU):
+        if u == NH1:
+            v.wait_ge(sem.ld13, 16)
+        v.wait_ge(sem["pe%d" % u], 1)
+        v.tensor_tensor(part(u), bank(u), tab(3, u), add).then_inc(sem["sv%d" % u], 1)
 
     sent = 0
-    for c in order[:-1]:
-        dsts = [2 * c, 2 * c + 1]
-        eng = _bits(topo.mask(core, T.cores[dsts[0]]) & topo.mask(core, T.cores[dsts[1]]))
-        half = len(eng) // 2
-        trs = []
-        for i, d in enumerate(dsts):
+    for u, trs in _plan(rank, T, topo):
+        calls = []
+        for d, es in trs:
             rid, pid = topo.addr(T.cores[d], core)
-            trs.append(RemoteDMATransfer(dst_ids=[DstId(rid=rid, pnc=pid)],
-                                         dma_engine_mask=_mask(eng[i * half:(i + 1) * half]),
-                                         remote_sem=sem["ar%d" % rank],
-                                         src=T.part[:, blk(d)], dst=T.land[:, blk(rank)]))
-            sent += half
-        g.wait_ge(sem["sv%d" % c], 1)
-        g.remote_dma_fused(trs, local_sem=sem.sent)
-    sib = rank ^ 1
-    rid, pid = topo.addr(T.cores[sib], core)
-    m = topo.mask(core, T.cores[sib])
-    g.wait_ge(sem["sv%d" % own], 1)
-    g.remote_dma(out_ap=T.land[:, blk(rank)], in_ap=T.part[:, blk(sib)], remote_sem=sem["ar%d" % rank],
-                 local_sem=sem.sent, pid=pid, routing_id=rid, dma_engine_mask=m)
-    sent += len(_bits(m))
+            calls.append(RemoteDMATransfer(dst_ids=[DstId(rid=rid, pnc=pid)], dma_engine_mask=_mask(es),
+                                           remote_sem=sem["ar%d" % rank],
+                                           src=T.part[:, blk(d)], dst=T.land[:, blk(rank)]))
+            sent += len(es)
+        g.wait_ge(sem["sv%d" % u], 1)
+        g.remote_dma_fused(calls, local_sem=sem.sent)
 
-    arrivals = []
-    for j in range(1, NCH):
-        cs = (own - j) % NCH
-        for s in (2 * cs, 2 * cs + 1):
-            e = _bits(topo.mask(T.cores[s], T.cores[2 * own]) & topo.mask(T.cores[s], T.cores[2 * own + 1]))
-            arrivals.append((s, len(e) // 2))
-    arrivals.append((sib, len(_bits(topo.mask(T.cores[sib], core)))))
-    run = T.ps[:, W:W + F]
-    v.wait_ge(sem["sv%d" % own], 1)
-    for i, (s, n) in enumerate(arrivals):
+    arrivals = sorted((_finish(_plan(s, T, topo))[rank], s) for s in range(N) if s != rank)
+    run = T.ps[:, off:off + F]
+    v.wait_ge(sem["sv%d" % (NU - 1)], 1)
+    for i, ((_t, n), s) in enumerate(arrivals):
         v.wait_ge(sem["ar%d" % s], n)
         if i:
             v.wait_ge(sem.vc, i)

from concourse.bass import DstId, RemoteDMATransfer
from concourse.mybir import AluOpType

N, K, F = 12, 4, 64
W = N * F
CH = 2 * F
NCH = N // 2
HP = NCH // 2
HW = HP * CH
BANK = 512
NU = 8
NV = 3
NH1 = 4
B = 32

SCRATCH = {
    "tab": ("sbuf", [128, K * W], "bfloat16"),
    "seed": ("sbuf", [128, B * B], "bfloat16"),
    "eye": ("sbuf", [128, 128], "bfloat16"),
    "part": ("sbuf", [128, W], "float32"),
    "land": ("sbuf", [128, W], "float32"),
    "acc": ("sbuf", [128, F], "float32"),
    "ps": ("psum", [128, (1 + NU - NV) * BANK], "float32"),
}

SEMAPHORES = (["ms", "ey", "sent", "vp", "vc", "st"]
              + ["ld%d%d" % (h, k) for h in range(2) for k in range(K)]
              + ["pe%d" % u for u in range(NU)]
              + ["sv%d" % u for u in range(NU)]
              + ["ar%d" % s for s in range(N)])


def _bits(m):
    return [e for e in range(m.bit_length()) if (m >> e) & 1]


def _mask(engines):
    m = 0
    for e in engines:
        m |= 1 << e
    return m


def _dests(rank):
    own = rank // 2
    mine, p = own // HP, own % HP
    far = [HP * (1 - mine) + (p + j) % HP for j in range(HP)]
    near = [HP * mine + (p + j) % HP for j in range(1, HP)]
    first = 2 * far[0] + rank % 2
    return ([[first], [first ^ 1]] + [[2 * c, 2 * c + 1] for c in far[1:] + near] + [[rank ^ 1], [rank]])


def _plan(rank, T, topo):
    core = T.cores[rank]
    m = None
    for d in range(N):
        if d != rank:
            m = topo.mask(core, T.cores[d]) if m is None else m & topo.mask(core, T.cores[d])
    eng = _bits(m)
    h = len(eng) // 2
    out = []
    for u, ds in enumerate(_dests(rank)[:-1]):
        out.append((u, [(ds[0], eng)] if len(ds) == 1 else [(ds[0], eng[:h]), (ds[1], eng[h:])]))
    return out


def _finish(plan):
    busy, out = {}, {}
    for _u, trs in plan:
        for d, es in trs:
            t = max(busy.get(e, 0) for e in es) + 128 // len(es)
            for e in es:
                busy[e] = t
            out[d] = (t, len(es))
    return out


def rank_program(g, core, T, topo):
    rank = T.rank_of(core)
    if rank is None:
        return
    v, pe, sy, sc, sem = g.vector, g.tensor, g.sync, g.scalar, T.sem
    add = AluOpType.add
    units = [(min(ds) * F, len(ds) * F) for ds in _dests(rank)]
    halves = [1 - (rank // 2) // HP, (rank // 2) // HP]

    def blk(r):
        return slice(r * F, (r + 1) * F)

    def tab(k, u):
        a, w = units[u]
        return T.tab[:, k * W + a:k * W + a + w]

    def part(u):
        a, w = units[u]
        return T.part[:, a:a + w]

    v.memset(T.seed[0:1, :], 0.0).then_inc(sem.ms, 1)
    v.memset(T.eye[:, :], 0.0).then_inc(sem.ms, 1)
    v.wait_ge(sem.ms, 2)
    v.memset(T.seed[0:1, 0:B * B:B + 1], 1.0).then_inc(sem.ms, 1)
    for i, h in enumerate(halves):
        for k in range(K):
            (sy, sc)[k % 2].dma_start(out=T.tab[:, k * W + h * HW:k * W + (h + 1) * HW],
                                      in_=T.gr[k, :, h * HW:(h + 1) * HW]).then_inc(sem["ld%d%d" % (i, k)], 16)
    sy.wait_ge(sem.ms, 3)
    sc.wait_ge(sem.ms, 3)
    nb = 128 // B
    for i in range(nb):
        (sy, sc)[i % 2].dma_start(out=T.eye[i * B:(i + 1) * B, i * B:(i + 1) * B],
                                  in_=T.seed[0:1, :]).then_inc(sem.ey, 16)

    def bank(u):
        a = (1 + u - NV) * BANK
        return T.ps[:, a:a + units[u][1]]

    pe.wait_ge(sem.ey, 16 * nb)
    for k in range(K - 1):
        pe.wait_ge(sem["ld0%d" % k], 16)
    for u in range(NV, NU):
        if u == NH1:
            for k in range(K - 1):
                pe.wait_ge(sem["ld1%d" % k], 16)
        for k in range(K - 1):
            mm = pe.matmul(bank(u), T.eye[:, :], tab(k, u), start=(k == 0), stop=(k == K - 2))
        mm.then_inc(sem["pe%d" % u], 1)

    nvp, off = 0, 0
    for u in range(NV):
        w = units[u][1]
        p = T.ps[:, off:off + w]
        off += w
        if u == 0:
            v.wait_ge(sem.ld00, 16)
            v.tensor_copy(p, tab(0, u)).then_inc(sem.vp, 1)
            nvp += 1
            v.wait_ge(sem.ld01, 16)
            v.wait_ge(sem.vp, nvp)
            v.tensor_tensor(p, p, tab(1, u), add).then_inc(sem.vp, 1)
        else:
            v.tensor_tensor(p, tab(0, u), tab(1, u), add).then_inc(sem.vp, 1)
        nvp += 1
        if u == 0:
            v.wait_ge(sem.ld02, 16)
        v.wait_ge(sem.vp, nvp)
        v.tensor_tensor(p, p, tab(2, u), add).then_inc(sem.vp, 1)
        nvp += 1
        if u == 0:
            v.wait_ge(sem.ld03, 16)
        v.wait_ge(sem.vp, nvp)
        v.tensor_tensor(part(u), p, tab(3, u), add).then_inc(sem["sv%d" % u], 1)
    for u in range(NV, NU):
        if u == NH1:
            v.wait_ge(sem.ld13, 16)
        v.wait_ge(sem["pe%d" % u], 1)
        v.tensor_tensor(part(u), bank(u), tab(3, u), add).then_inc(sem["sv%d" % u], 1)

    sent = 0
    for u, trs in _plan(rank, T, topo):
        calls = []
        for d, es in trs:
            rid, pid = topo.addr(T.cores[d], core)
            calls.append(RemoteDMATransfer(dst_ids=[DstId(rid=rid, pnc=pid)], dma_engine_mask=_mask(es),
                                           remote_sem=sem["ar%d" % rank],
                                           src=T.part[:, blk(d)], dst=T.land[:, blk(rank)]))
            sent += len(es)
        g.wait_ge(sem["sv%d" % u], 1)
        g.remote_dma_fused(calls, local_sem=sem.sent)

    arrivals = sorted((_finish(_plan(s, T, topo))[rank], s) for s in range(N) if s != rank)
    run = T.ps[:, off:off + F]
    v.wait_ge(sem["sv%d" % (NU - 1)], 1)
    for i, ((_t, n), s) in enumerate(arrivals):
        v.wait_ge(sem["ar%d" % s], n)
        if i:
            v.wait_ge(sem.vc, i)
        v.tensor_tensor(T.acc[:, :] if i == len(arrivals) - 1 else run, run if i else T.part[:, blk(rank)],
                        T.land[:, blk(s)], add).then_inc(sem.vc, 1)
    sy.wait_ge(sem.vc, len(arrivals))
    sy.dma_start(out=T.y[:, :], in_=T.acc[:, :]).then_inc(sem.st, 16)
    sy.wait_ge(sem.st, 16)
    g.wait_ge(sem.sent, sent)
